import numpy as np
import ml_dtypes


def mxq(x, axis, fmt="e4m3"):
    dtype, down = {"e4m3": (ml_dtypes.float8_e4m3fn, 7), "e5m2": (ml_dtypes.float8_e5m2, 14)}[fmt]
    v = np.moveaxis(np.asarray(x, np.float32).astype(ml_dtypes.bfloat16).astype(np.float64), axis, -1)
    blocks = v.reshape(v.shape[:-1] + (-1, 32))
    amax = np.abs(blocks).max(-1, keepdims=True)
    byte = np.maximum(np.where(amax > 0, np.frexp(amax)[1] - 1 + 127, 0) - down, 1)
    scale = np.exp2(byte - 127.0)
    codes = (blocks / scale).astype(np.float32).astype(dtype).astype(np.float64)
    return np.moveaxis((codes * scale).reshape(v.shape), -1, axis)


WIDE = False


def mx_kscale(k):
    if not WIDE:
        return np.ones(k)
    levels = np.array([10, -10, 5, -5, 0])
    if k % 512:
        return np.exp2(np.random.permutation(np.resize(levels, k // 32))).repeat(32)
    a = np.empty((k // 512, 16))
    for p in range(k // 512):
        a[p, :8] = np.random.permutation(np.resize(levels, 8))
        for g in range(8):
            far = levels[np.abs(levels - a[p, g]) >= 10]
            a[p, g + 8] = far[np.random.randint(len(far))]
    return np.exp2(a.ravel()).repeat(32)


def f64(x):
    return np.asarray(x).astype(np.float64)


def striped(idx):
    return np.tile(idx.reshape(-1, 16).T, (8, 1)).astype(np.uint16)


def unstriped(offs):
    return offs[:16].T.reshape(-1).astype(np.int64)


def pack_weight(w):
    k, n = w.shape
    w = f64(np.asarray(w, np.float32).astype(ml_dtypes.bfloat16)).reshape(k // 32, 32, n)
    amax = np.abs(w).max(1)
    byte = np.clip(np.where(amax > 0, np.frexp(amax)[1] - 1 + 127 - 7, 1), 1, 254)
    scaled = (w * np.exp2(127.0 - byte)[:, None, :]).reshape(k, n).astype(np.float32)
    words = np.ascontiguousarray(scaled.reshape(k // 512, 128, 4, n).transpose(0, 1, 3, 2)).astype(ml_dtypes.float8_e4m3fn).view(np.uint8)
    return words, np.ascontiguousarray(byte.astype(np.uint8).reshape(k // 512, 16, n))


def unpack_weight(words, scales):
    g, p, n, _ = words.shape
    vals = np.ascontiguousarray(words).view(ml_dtypes.float8_e4m3fn).astype(np.float64) * np.repeat(np.exp2(scales.astype(np.float64) - 127.0), 8, axis=1)[..., None]
    return vals.transpose(0, 1, 3, 2).reshape(g * 512, n)


E2M1 = np.array([0.0, 0.5, 1.0, 1.5, 2.0, 3.0, 4.0, 6.0, -0.0, -0.5, -1.0, -1.5, -2.0, -3.0, -4.0, -6.0])


def pack_fp4(w):
    k, n = w.shape
    w = f64(np.asarray(w, np.float32).astype(ml_dtypes.bfloat16)).reshape(k // 32, 32, n)
    amax = np.abs(w).max(1)
    mant, ex = np.frexp(amax / 6.0)
    byte = np.clip(np.where(amax > 0, np.where(mant > 0.5, ex, ex - 1) + 127, 1), 1, 254)
    scaled = (w * np.exp2(127.0 - byte)[:, None, :]).reshape(k, n).astype(np.float32)
    c = np.ascontiguousarray(scaled.reshape(k // 512, 128, 4, n).transpose(0, 1, 3, 2)).astype(ml_dtypes.float4_e2m1fn).view(np.uint8) & 0xF
    words = (c[..., 0::2] | (c[..., 1::2] << 4)).reshape(k // 512, 128, 2 * n)
    return np.ascontiguousarray(words), np.ascontiguousarray(byte.astype(np.uint8).reshape(k // 512, 16, n))


def unpack_fp4(words, scales):
    g, _, n = scales.shape
    words = np.ascontiguousarray(words).reshape(g, 128, n, 2)
    nib = np.empty((g, 128, n, 4), np.uint8)
    nib[..., 0::2] = words & 0xF
    nib[..., 1::2] = words >> 4
    vals = E2M1[nib] * np.repeat(np.exp2(scales.astype(np.float64) - 127.0), 8, axis=1)[..., None]
    return vals.transpose(0, 1, 3, 2).reshape(g * 512, n)


def relu(v):
    return np.maximum(v, 0.0)


def sigmoid(v):
    return 1.0 / (1.0 + np.exp(-np.maximum(v, -700.0)))


K, T, S, D, N, H = 512, 4096, 1024, 4, 128, 512


def setup_inputs():
    n = np.random.standard_normal
    s = mx_kscale(K)[:, None]
    u = mx_kscale(H)
    packed_xT = pack_weight(n((K, T)) * s)
    packed_w1 = pack_fp4(n((K, H)) / np.sqrt(K) / s)
    packed_w2 = pack_fp4(n((K, H)) / np.sqrt(K) / s)
    packed_w3 = pack_fp4(n((H, N)) / np.sqrt(H) / u[:, None])
    return {
        "x_words": packed_xT[0],
        "x_scales": packed_xT[1],
        "w1_words": packed_w1[0],
        "w1_scales": packed_w1[1],
        "w2_words": packed_w2[0],
        "w2_scales": packed_w2[1],
        "cut": (np.random.uniform(-0.5, 0.7, (H, S))).astype(np.float32),
        "seat": (np.random.uniform(0.5, 1.5, (H, S))).astype(np.float32),
        "unit": (np.random.uniform(0.6, 1.4, (H, 1)) * u[:, None]).astype(np.float32),
        "w3_words": packed_w3[0],
        "w3_scales": packed_w3[1],
        "offs": striped(np.random.permutation(T)[:S]),
        "sch": striped(np.random.permutation(S)),
    }


def reference(x_words, x_scales, w1_words, w1_scales, w2_words, w2_scales, cut, seat, unit, w3_words, w3_scales, offs, sch):
    xq = unpack_weight(x_words, x_scales)[:, unstriped(offs)]
    sc = unpack_fp4(w1_words, w1_scales).T @ xq
    adm = sigmoid(3.0 * (sc - f64(cut)))
    ut = unpack_fp4(w2_words, w2_scales).T @ xq
    eu = adm * (np.exp(0.9 * np.tanh(ut)))
    tot = eu.reshape(len(eu), -1, D).sum(axis=2)
    chs = eu / (np.repeat(tot, D, axis=1) + 0.5)
    cs = chs[:, unstriped(sch)]
    scs = sc[:, unstriped(sch)]
    fill = cs.reshape(len(cs), -1, D).sum(axis=2)
    press = relu(scs + np.repeat(fill, D, axis=1) - f64(seat))
    hid = f64(unit) * (cs - (0.3 * press))
    return unpack_fp4(w3_words, w3_scales).T @ mxq(hid, 0, "e4m3")

@@ -1,0 +1,302 @@
+import math
+from contextlib import ExitStack
+
+import concourse.mybir as mybir
+from concourse.masks import make_identity
+
+K, T, S, D, N, H = 512, 4096, 1024, 4, 128, 512
+FLOPS = 2 * K * H * S * 2 + 2 * H * N * S
+
+F32 = mybir.dt.float32
+BF16 = mybir.dt.bfloat16
+I32 = mybir.dt.int32
+U32 = mybir.dt.uint32
+U16 = mybir.dt.uint16
+U8 = mybir.dt.uint8
+FP8X4 = mybir.dt.float8_e4m3fn_x4
+FP4X4 = mybir.dt.float4_e2m1fn_x4
+ALU = mybir.AluOpType
+ACT = mybir.ActivationFunctionType
+
+P = 128
+PACK = 4
+HALF = 512
+CHUNKS = (256, 256, 256, 128, 128)
+PRESS = 0.3
+
+PE_TOT = True
+PE_FILL = True
+NEWTON = True
+
+LOG_SLACK = math.log(1.0 / math.log(2.0)) / math.log(2.0) + 1.0 - 1.0 / math.log(2.0)
+SEED_SCALE = -math.log(2.0) / 2.0**23
+SEED_BIAS = math.log(2.0) * (127.0 - LOG_SLACK / 2.0)
+MID = (2.0 ** (LOG_SLACK / 2.0) + 2.0 ** (-LOG_SLACK / 2.0)) / 2.0
+RAD = (2.0 ** (LOG_SLACK / 2.0) - 2.0 ** (-LOG_SLACK / 2.0)) / 2.0
+CHEB = 4.0 * (MID / RAD) ** 3 - 3.0 * MID / RAD
+QUAD_SCALE = math.sqrt(4.0 / (RAD**3 * CHEB))
+QUAD_BIAS = -1.5 * MID * QUAD_SCALE
+QUAD_ADD = (12.0 * MID**2 / RAD**3 - 3.0 / RAD) / CHEB - QUAD_BIAS**2
+
+
+def load_scale_rows(queue, plane, scales):
+    for q in range(4):
+        queue.dma_start(out=plane[32 * q : 32 * q + 4, :].bitcast(I32), in_=scales[0, 4 * q : 4 * q + 4, :].bitcast(I32))
+
+
+def tile_picked_yschch_net_p_kernel(
+    tc, x_words, x_scales, w1_words, w1_scales, w2_words, w2_scales, cut, seat, unit, w3_words, w3_scales, offs, sch, out
+):
+    nc = tc.nc
+    with ExitStack() as ctx:
+        keep = ctx.enter_context(tc.tile_pool(name="keep", bufs=1))
+        work = ctx.enter_context(tc.tile_pool(name="work", bufs=3))
+        small = ctx.enter_context(tc.tile_pool(name="small", bufs=2))
+        psum = ctx.enter_context(tc.psum_pool(name="psum", bufs=2))
+
+        offs_sb = keep.tile([P, S // 16], U16, name="offs_sb")
+        sch_sb = keep.tile([P, S // 16], U16, name="sch_sb")
+        xw = keep.tile([P, T], U32, name="xw")
+        xs = keep.tile([P, T], U8, name="xs")
+        w_raw = [keep.tile([P, 2 * H], U8, name="w_raw%d" % a, tag="slot%d" % a) for a in range(2)]
+        ws_raw = [keep.tile([P, H], U8, name="ws_raw%d" % a, tag="slot%d" % (3 - a)) for a in range(2)]
+        w_dealt = [keep.tile([P, 2 * H], U8, name="w_dealt%d" % a, align_bytes=64) for a in range(2)]
+        ws_dealt = [keep.tile([P, H], U8, name="ws_dealt%d" % a, align_bytes=64) for a in range(2)]
+        gain = keep.tile([P, PACK], F32, name="gain")
+
+        nc.vector.memset(xs[:].bitcast(I32), 0)
+        nc.vector.memset(ws_raw[1][:].bitcast(I32), 0)
+        nc.gpsimd.memset(ws_raw[0][:].bitcast(I32), 0)
+
+        nc.sync.dma_start(offs_sb[:], offs)
+        nc.sync.dma_start(sch_sb[:], sch)
+        for a, words in enumerate((w1_words, w2_words)):
+            nc.sync.dma_start(out=w_raw[a][:].bitcast(I32), in_=words[0].bitcast(I32))
+        nc.sync.dma_start(out=xw[:].bitcast(I32), in_=x_words[0].rearrange("p n t -> p (n t)").bitcast(I32))
+        load_scale_rows(nc.gpsimd, ws_raw[0], w1_scales)
+        load_scale_rows(nc.scalar, xs, x_scales)
+        load_scale_rows(nc.sync, ws_raw[1], w2_scales)
+        starts = [sum(CHUNKS[:c]) for c in range(len(CHUNKS))]
+
+        for a in range(2):
+            nc.vector.tensor_copy(
+                out=w_dealt[a][:].rearrange("p (t m b) -> p t m b", t=PACK, b=2),
+                in_=w_raw[a][:].rearrange("p (m t b) -> p t m b", t=PACK, b=2),
+            )
+        xq, xb = [], []
+        for h in range(S // HALF):
+            cols = offs_sb[:, h * HALF // 16 : (h + 1) * HALF // 16]
+            scale_bytes = keep.tile([P, HALF], U8, name="xb%d" % h, align_bytes=64)
+            nc.vector.tensor_copy(scale_bytes[:], xs[:].indirect(cols))
+            xb.append(scale_bytes)
+        for a in range(2):
+            nc.vector.tensor_copy(
+                out=ws_dealt[a][:].rearrange("p (t m) -> p t m", t=PACK),
+                in_=ws_raw[a][:].rearrange("p (m t) -> p t m", t=PACK),
+            )
+        for h in range(S // HALF):
+            cols = offs_sb[:, h * HALF // 16 : (h + 1) * HALF // 16]
+            words = keep.tile([P, HALF], U32, name="xq%d" % h, align_bytes=64)
+            nc.vector.tensor_copy(words[:], xw[:].indirect(cols))
+            xq.append(words)
+
+        ident = keep.tile([P, P], F32, name="ident", tag="slot3")
+        make_identity(nc, ident[:])
+        SPANS = ((0, 1), (1, 2), (2, 4))
+        cut_rows = cut.rearrange("(p t) j -> p t j", t=PACK)
+        cut_sb = []
+        for k, (lo, hi) in enumerate(SPANS):
+            tile = keep.tile([P, hi - lo, S], F32, name="cut%d" % k, tag="slot%d" % k)
+            nc.sync.dma_start(out=tile[:], in_=cut_rows[:, lo:hi, :])
+            cut_sb.extend(tile[:, t, :] for t in range(hi - lo))
+        seat_rows = seat.rearrange("(p t) j -> p t j", t=PACK)
+        seat_sb = {}
+        QUARTER = S // PACK
+
+        def load_seats(k):
+            lo, hi = SPANS[k][0] * QUARTER, SPANS[k][1] * QUARTER
+            tile = keep.tile([P, PACK, hi - lo], F32, name="seat%d" % k, tag="slot%d" % k)
+            nc.sync.dma_start(out=tile[:], in_=seat_rows[:, :, lo:hi])
+            for c, n in enumerate(CHUNKS):
+                if lo <= starts[c] < hi:
+                    seat_sb[c] = tile[:, :, starts[c] - lo : starts[c] - lo + n]
+
+        def product(a, t, h, tag):
+            acc = psum.tile([P, HALF], F32, name=tag)
+            nc.tensor.matmul_mx(
+                out=acc[:],
+                lhsT=w_dealt[a][:, 2 * P * t : 2 * P * (t + 1)].bitcast(FP4X4),
+                lhsT_scale=ws_dealt[a][:, P * t : P * (t + 1)],
+                rhs=xq[h][:].bitcast(FP8X4),
+                rhs_scale=xb[h][:],
+                start=True,
+                stop=True,
+            )
+            return acc
+
+        def turned_group_sums(values, groups):
+            turned = psum.tile([P, HALF], F32, name="turned")
+            for b in range(groups // P):
+                for d in range(D):
+                    nc.tensor.matmul(
+                        turned[:, P * b : P * (b + 1)],
+                        lhsT=values[:, D * P * b + d : D * P * (b + 1) : D],
+                        rhs=ident[:],
+                        is_transpose=True,
+                        start=(d == 0),
+                        stop=(d == D - 1),
+                    )
+            return turned[:, :groups]
+
+        def turn_back(values, groups):
+            back = psum.tile([P, HALF], F32, name="back")
+            for b in range(groups // P):
+                nc.tensor.transpose(back[:, P * b : P * (b + 1)], values[:, P * b : P * (b + 1)], ident[:])
+            return back[:, :groups]
+
+        def vector_group_sums(dst, values, groups, add):
+            pairs = small.tile([P, 2 * (S // D)], F32, name="pairs")
+            v = values.rearrange("p (v d) -> p v d", d=D)
+            pv = pairs[:, : 2 * groups].rearrange("p (v e) -> p v e", e=2)
+            nc.vector.tensor_tensor(pv, v[:, :, 0:2], v[:, :, 2:4], ALU.add)
+            nc.vector.scalar_tensor_tensor(dst, pv[:, :, 0], add, pv[:, :, 1], ALU.add, ALU.add)
+
+        sc_sb = [keep.tile([P, S], F32, name="sc%d" % t) for t in range(PACK)]
+        chs_sb = [keep.tile([P, S], F32, name="chs%d" % t) for t in range(PACK)]
+        eu_sb = [None] * PACK
+        G = S // D
+
+        def scores(t, h):
+            cols = slice(h * HALF, (h + 1) * HALF)
+            if h == 0:
+                eu_sb[t] = small.tile([P, S], F32, name="eu")
+            sc_ps = product(0, t, h, "sc_ps")
+            ut_ps = product(1, t, h, "ut_ps")
+            z = work.tile([P, HALF], F32, name="z")
+            nc.vector.tensor_tensor(z[:], sc_ps[:], cut_sb[t][:, cols], ALU.subtract)
+            tu = work.tile([P, HALF], F32, name="tu")
+            nc.scalar.activation(tu[:], ut_ps[:], ACT.Tanh)
+            e = work.tile([P, HALF], F32, name="e")
+            nc.scalar.activation(e[:], tu[:], ACT.Exp, scale=0.9)
+            th = work.tile([P, HALF], F32, name="th")
+            nc.scalar.activation(th[:], z[:], ACT.Tanh, scale=1.5)
+            nc.scalar.copy(sc_sb[t][:, cols], sc_ps[:])
+            nc.vector.scalar_tensor_tensor(eu_sb[t][:, cols], th[:], 1.0, e[:], ALU.add, ALU.mult)
+
+        def choices(t):
+            den = small.tile([P, G], F32, name="den")
+            if PE_TOT:
+                nc.scalar.activation(den[:], turned_group_sums(eu_sb[t][:], G), ACT.Identity, bias=1.0)
+            else:
+                vector_group_sums(den[:], eu_sb[t][:], G, 1.0)
+            rec = small.tile([P, G], F32, name="rec")
+            if NEWTON:
+                y0 = small.tile([P, G], F32, name="y0")
+                nc.scalar.activation(y0[:], den[:].bitcast(U32), ACT.Exp, scale=SEED_SCALE, bias=SEED_BIAS)
+                t0 = small.tile([P, G], F32, name="t0")
+                nc.vector.tensor_tensor(t0[:], den[:], y0[:], ALU.mult)
+                q = small.tile([P, G], F32, name="q")
+                nc.scalar.activation(q[:], t0[:], ACT.Square, scale=QUAD_SCALE, bias=QUAD_BIAS)
+                y1 = small.tile([P, G], F32, name="y1")
+                nc.vector.scalar_tensor_tensor(y1[:], q[:], QUAD_ADD, y0[:], ALU.add, ALU.mult)
+                t1 = small.tile([P, G], F32, name="t1")
+                nc.vector.tensor_tensor(t1[:], den[:], y1[:], ALU.mult)
+                nc.vector.scalar_tensor_tensor(rec[:], t1[:], 2.0, y1[:], ALU.subtract, ALU.mult)
+                factor = -1.0 / PRESS
+            else:
+                nc.vector.reciprocal(rec[:], den[:])
+                factor = 1.0 / PRESS
+            rr = turn_back(rec[:], G) if PE_TOT else rec[:]
+            nc.vector.scalar_tensor_tensor(
+                chs_sb[t][:].rearrange("p (v d) -> p v d", d=D),
+                eu_sb[t][:].rearrange("p (v d) -> p v d", d=D),
+                factor,
+                rr.unsqueeze(2).to_broadcast([P, G, D]),
+                ALU.mult,
+                ALU.mult,
+            )
+
+        cs_sb = [keep.tile([P, PACK * n], F32, name="cs%d" % c) for c, n in enumerate(CHUNKS)]
+        gap_sb = [keep.tile([P, PACK * n], F32, name="gap%d" % c) for c, n in enumerate(CHUNKS)]
+
+        def sch_cols(c):
+            return sch_sb[:, starts[c] // 16 : (starts[c] + CHUNKS[c]) // 16]
+
+        def fetch_scores(t, c):
+            n = CHUNKS[c]
+            nc.vector.tensor_tensor(
+                gap_sb[c][:, t * n : (t + 1) * n], sc_sb[t][:].indirect(sch_cols(c)), seat_sb[c][:, t, :], ALU.subtract
+            )
+
+        def fetch_choices(t, c):
+            n = CHUNKS[c]
+            nc.scalar.activation(cs_sb[c][:, t * n : (t + 1) * n], chs_sb[t][:].indirect(sch_cols(c)), ACT.Copy)
+
+        def pressure(c):
+            n = CHUNKS[c]
+            fill = small.tile([P, G], F32, name="fill")
+            if PE_FILL:
+                nc.scalar.copy(fill[:, :n], turned_group_sums(cs_sb[c][:], n))
+                ff = turn_back(fill[:, :n], n)
+            else:
+                vector_group_sums(fill[:, :n], cs_sb[c][:], n, 0.0)
+                ff = fill[:, :n]
+            gap = gap_sb[c][:].rearrange("p (v d) -> p v d", d=D)
+            nc.vector.scalar_tensor_tensor(gap, ff.unsqueeze(2).to_broadcast([P, n, D]), PRESS, gap, ALU.mult, ALU.add)
+            nc.vector.scalar_tensor_tensor(gap_sb[c][:], gap_sb[c][:], 0.0, cs_sb[c][:], ALU.max, ALU.subtract)
+
+        def districts(c):
+            n = CHUNKS[c]
+            hid = small.tile([P, PACK, 256], BF16, name="hid")
+            for t in range(PACK):
+                nc.scalar.activation(hid[:, t, :n], gap_sb[c][:, t * n : (t + 1) * n], ACT.Copy, scale=gain[:, t : t + 1])
+            woven = small.tile([P, 256, PACK], BF16, name="woven", align_bytes=64)
+            nc.vector.tensor_copy(
+                out=woven[:, :n, :].rearrange("p (c i) t -> p c t i", i=4),
+                in_=hid[:, :, :n].rearrange("p t (c i) -> p c t i", i=4),
+            )
+            codes = small.tile([P, 256], U32, name="codes", align_bytes=64)
+            plane = small.tile([P, 256], U8, name="plane", align_bytes=64)
+            nc.vector.quantize_mx(
+                out=codes[:, :n].bitcast(FP8X4), scales=plane[:, :n], in_=woven[:, :n, :].rearrange("p j t -> p (j t)")
+            )
+            acc = psum.tile([P, HALF], F32, name="sc_ps")
+            nc.tensor.matmul_mx(
+                out=acc[:, :n],
+                lhsT=w3w[:].bitcast(FP4X4),
+                lhsT_scale=w3s[:],
+                rhs=codes[:, :n].bitcast(FP8X4),
+                rhs_scale=plane[:, :n],
+                start=True,
+                stop=True,
+            )
+            res = small.tile([P, 256], F32, name="res")
+            nc.scalar.copy(res[:, :n], acc[:, :n])
+            nc.sync.dma_start(out=out[:, starts[c] : starts[c] + n], in_=res[:, :n])
+
+        for t in range(PACK + 1):
+            if t < PACK:
+                scores(t, 0)
+            if t >= 1:
+                choices(t - 1)
+            if t < PACK:
+                scores(t, 1)
+                for k, span in enumerate(SPANS):
+                    if span[1] == t + 1:
+                        load_seats(k)
+        w3w = keep.tile([P, 2 * N], U8, name="w3w", tag="w_dealt0", align_bytes=64)
+        w3s = keep.tile([P, N], U8, name="w3s", tag="ws_dealt0", align_bytes=64)
+        unit_sb = keep.tile([P, PACK], F32, name="unit_sb", tag="w_dealt1", align_bytes=64)
+        nc.gpsimd.memset(w3s[:].bitcast(I32), 0)
+        nc.sync.dma_start(out=unit_sb[:], in_=unit.rearrange("(p t) o -> p (t o)", t=PACK))
+        nc.sync.dma_start(out=w3w[:].bitcast(I32), in_=w3_words[0].bitcast(I32))
+        load_scale_rows(nc.sync, w3s, w3_scales)
+        nc.vector.tensor_scalar(gain[:], unit_sb[:], -PRESS, None, ALU.mult)
+        for c in range(len(CHUNKS) + 1):
+            if c < len(CHUNKS):
+                for t in range(PACK):
+                    fetch_scores(t, c)
+                    fetch_choices(t, c)
+                pressure(c)
+            if c >= 1:
+                districts(c - 1)

@@ -21,9 +21,24 @@ ACT = mybir.ActivationFunctionType
 P = 128
 PACK = 4
 HALF = 512
-CHUNKS = (256, 256, 256, 128, 128)
+CHUNKS = (256,256,256,256)
 PRESS = 0.3
 
+GAPB = 4
+CSB = 3
+EUB = 3
+PSA = (2,2,2,2)
+NV = 2
+NU = 0
+TM = 2
+L1 = 0
+L2 = 3
+L3 = 5
+L4 = 8
+PERHALF = False
+WB = 3
+SB = 4
+WEAVE_S = (0,)
 PE_TOT = True
 PE_FILL = True
 NEWTON = True
@@ -39,8 +54,8 @@ QUAD_BIAS = -1.5 * MID * QUAD_SCALE
 QUAD_ADD = (12.0 * MID**2 / RAD**3 - 3.0 / RAD) / CHEB - QUAD_BIAS**2
 
 
-def load_scale_rows(queue, plane, scales):
-    for q in range(4):
+def load_scale_rows(queues, plane, scales):
+    for q, queue in enumerate(queues):
         queue.dma_start(out=plane[32 * q : 32 * q + 4, :].bitcast(I32), in_=scales[0, 4 * q : 4 * q + 4, :].bitcast(I32))
 
 
@@ -50,32 +65,33 @@ def tile_picked_yschch_net_p_kernel(
     nc = tc.nc
     with ExitStack() as ctx:
         keep = ctx.enter_context(tc.tile_pool(name="keep", bufs=1))
-        work = ctx.enter_context(tc.tile_pool(name="work", bufs=3))
-        small = ctx.enter_context(tc.tile_pool(name="small", bufs=2))
+        work = ctx.enter_context(tc.tile_pool(name="work", bufs=WB))
+        small = ctx.enter_context(tc.tile_pool(name="small", bufs=SB))
         psum = ctx.enter_context(tc.psum_pool(name="psum", bufs=2))
 
         offs_sb = keep.tile([P, S // 16], U16, name="offs_sb")
         sch_sb = keep.tile([P, S // 16], U16, name="sch_sb")
         xw = keep.tile([P, T], U32, name="xw")
-        xs = keep.tile([P, T], U8, name="xs")
+        xs = keep.tile([P, T], U8, name="xs", tag="xq", align_bytes=64)
         w_raw = [keep.tile([P, 2 * H], U8, name="w_raw%d" % a, tag="slot%d" % a) for a in range(2)]
-        ws_raw = [keep.tile([P, H], U8, name="ws_raw%d" % a, tag="slot%d" % (3 - a)) for a in range(2)]
+        ws_raw = [keep.tile([P, H], U8, name="ws_raw0", tag="slot2"), keep.tile([P, H], U8, name="ws_raw1", tag="xb0", align_bytes=64)]
         w_dealt = [keep.tile([P, 2 * H], U8, name="w_dealt%d" % a, align_bytes=64) for a in range(2)]
         ws_dealt = [keep.tile([P, H], U8, name="ws_dealt%d" % a, align_bytes=64) for a in range(2)]
-        gain = keep.tile([P, PACK], F32, name="gain")
 
         nc.vector.memset(xs[:].bitcast(I32), 0)
-        nc.vector.memset(ws_raw[1][:].bitcast(I32), 0)
+        nc.gpsimd.memset(ws_raw[1][:].bitcast(I32), 0)
         nc.gpsimd.memset(ws_raw[0][:].bitcast(I32), 0)
 
         nc.sync.dma_start(offs_sb[:], offs)
         nc.sync.dma_start(sch_sb[:], sch)
+        unit_sb = keep.tile([P, PACK], F32, name="unit_sb", tag="slot3")
+        nc.sync.dma_start(out=unit_sb[:], in_=unit.rearrange("(p t) o -> p (t o)", t=PACK))
         for a, words in enumerate((w1_words, w2_words)):
             nc.sync.dma_start(out=w_raw[a][:].bitcast(I32), in_=words[0].bitcast(I32))
         nc.sync.dma_start(out=xw[:].bitcast(I32), in_=x_words[0].rearrange("p n t -> p (n t)").bitcast(I32))
-        load_scale_rows(nc.gpsimd, ws_raw[0], w1_scales)
-        load_scale_rows(nc.scalar, xs, x_scales)
-        load_scale_rows(nc.sync, ws_raw[1], w2_scales)
+        load_scale_rows([nc.scalar] * 4, xs, x_scales)
+        load_scale_rows([nc.gpsimd] + [nc.scalar] * 3, ws_raw[1], w2_scales)
+        load_scale_rows([nc.gpsimd] * 4, ws_raw[0], w1_scales)
         starts = [sum(CHUNKS[:c]) for c in range(len(CHUNKS))]
 
         for a in range(2):
@@ -83,46 +99,53 @@ def tile_picked_yschch_net_p_kernel(
                 out=w_dealt[a][:].rearrange("p (t m b) -> p t m b", t=PACK, b=2),
                 in_=w_raw[a][:].rearrange("p (m t b) -> p t m b", t=PACK, b=2),
             )
+
+        gain = keep.tile([P, PACK], F32, name="gain", tag="slot1")
+        nc.scalar.activation(gain[:], unit_sb[:], ACT.Copy, scale=-PRESS)
+
+        def deal_scales(a):
+            nc.vector.tensor_copy(
+                out=ws_dealt[a][:].rearrange("p (t m) -> p t m", t=PACK),
+                in_=ws_raw[a][:].rearrange("p (m t) -> p t m", t=PACK),
+            )
+
+        deal_scales(1)
         xq, xb = [], []
         for h in range(S // HALF):
             cols = offs_sb[:, h * HALF // 16 : (h + 1) * HALF // 16]
             scale_bytes = keep.tile([P, HALF], U8, name="xb%d" % h, align_bytes=64)
             nc.vector.tensor_copy(scale_bytes[:], xs[:].indirect(cols))
             xb.append(scale_bytes)
-        for a in range(2):
-            nc.vector.tensor_copy(
-                out=ws_dealt[a][:].rearrange("p (t m) -> p t m", t=PACK),
-                in_=ws_raw[a][:].rearrange("p (m t) -> p t m", t=PACK),
-            )
+        xq_all = keep.tile([P, S], U32, name="xq", align_bytes=64)
         for h in range(S // HALF):
             cols = offs_sb[:, h * HALF // 16 : (h + 1) * HALF // 16]
-            words = keep.tile([P, HALF], U32, name="xq%d" % h, align_bytes=64)
-            nc.vector.tensor_copy(words[:], xw[:].indirect(cols))
+            words = xq_all[:, h * HALF : (h + 1) * HALF]
+            nc.vector.tensor_copy(words, xw[:].indirect(cols))
             xq.append(words)
+            if h == 0:
+                deal_scales(0)
 
-        ident = keep.tile([P, P], F32, name="ident", tag="slot3")
+        ident = keep.tile([P, P], F32, name="ident", tag="slot0")
         make_identity(nc, ident[:])
-        SPANS = ((0, 1), (1, 2), (2, 4))
+        SPANS = ((0, 2), (2, 4))
         cut_rows = cut.rearrange("(p t) j -> p t j", t=PACK)
         cut_sb = []
         for k, (lo, hi) in enumerate(SPANS):
-            tile = keep.tile([P, hi - lo, S], F32, name="cut%d" % k, tag="slot%d" % k)
+            tile = keep.tile([P, hi - lo, S], F32, name="cut%d" % k, tag=("slot3", "xw")[k])
             nc.sync.dma_start(out=tile[:], in_=cut_rows[:, lo:hi, :])
             cut_sb.extend(tile[:, t, :] for t in range(hi - lo))
         seat_rows = seat.rearrange("(p t) j -> p t j", t=PACK)
-        seat_sb = {}
-        QUARTER = S // PACK
+        seat_sb = []
 
-        def load_seats(k):
-            lo, hi = SPANS[k][0] * QUARTER, SPANS[k][1] * QUARTER
-            tile = keep.tile([P, PACK, hi - lo], F32, name="seat%d" % k, tag="slot%d" % k)
-            nc.sync.dma_start(out=tile[:], in_=seat_rows[:, :, lo:hi])
-            for c, n in enumerate(CHUNKS):
-                if lo <= starts[c] < hi:
-                    seat_sb[c] = tile[:, :, starts[c] - lo : starts[c] - lo + n]
+        def load_seats(lo, hi, tag):
+            tile = keep.tile([P, hi - lo, S], F32, name="seat%d" % lo, tag=tag)
+            nc.sync.dma_start(out=tile[:], in_=seat_rows[:, lo:hi, :])
+            seat_sb.extend(tile[:, t, :] for t in range(hi - lo))
+
+        load_seats(0, 4, "slot2")
 
         def product(a, t, h, tag):
-            acc = psum.tile([P, HALF], F32, name=tag)
+            acc = psum.tile([P, HALF], F32, name=tag, bufs=PSA[a])
             nc.tensor.matmul_mx(
                 out=acc[:],
                 lhsT=w_dealt[a][:, 2 * P * t : 2 * P * (t + 1)].bitcast(FP4X4),
@@ -135,7 +158,7 @@ def tile_picked_yschch_net_p_kernel(
             return acc
 
         def turned_group_sums(values, groups):
-            turned = psum.tile([P, HALF], F32, name="turned")
+            turned = psum.tile([P, HALF], F32, name="turned", bufs=PSA[2])
             for b in range(groups // P):
                 for d in range(D):
                     nc.tensor.matmul(
@@ -149,7 +172,7 @@ def tile_picked_yschch_net_p_kernel(
             return turned[:, :groups]
 
         def turn_back(values, groups):
-            back = psum.tile([P, HALF], F32, name="back")
+            back = psum.tile([P, HALF], F32, name="back", bufs=PSA[3])
             for b in range(groups // P):
                 nc.tensor.transpose(back[:, P * b : P * (b + 1)], values[:, P * b : P * (b + 1)], ident[:])
             return back[:, :groups]
@@ -169,9 +192,9 @@ def tile_picked_yschch_net_p_kernel(
         def scores(t, h):
             cols = slice(h * HALF, (h + 1) * HALF)
             if h == 0:
-                eu_sb[t] = small.tile([P, S], F32, name="eu")
-            sc_ps = product(0, t, h, "sc_ps")
+                eu_sb[t] = small.tile([P, S], F32, name="eu", bufs=EUB)
             ut_ps = product(1, t, h, "ut_ps")
+            sc_ps = product(0, t, h, "sc_ps")
             z = work.tile([P, HALF], F32, name="z")
             nc.vector.tensor_tensor(z[:], sc_ps[:], cut_sb[t][:, cols], ALU.subtract)
             tu = work.tile([P, HALF], F32, name="tu")
@@ -180,15 +203,16 @@ def tile_picked_yschch_net_p_kernel(
             nc.scalar.activation(e[:], tu[:], ACT.Exp, scale=0.9)
             th = work.tile([P, HALF], F32, name="th")
             nc.scalar.activation(th[:], z[:], ACT.Tanh, scale=1.5)
-            nc.scalar.copy(sc_sb[t][:, cols], sc_ps[:])
+            (nc.vector.tensor_copy if 2 * t + h < NV else nc.scalar.copy)(sc_sb[t][:, cols], sc_ps[:])
             nc.vector.scalar_tensor_tensor(eu_sb[t][:, cols], th[:], 1.0, e[:], ALU.add, ALU.mult)
 
-        def choices(t):
+        def choices(t, lo, G):
+            cols = slice(lo * D, (lo + G) * D)
             den = small.tile([P, G], F32, name="den")
             if PE_TOT:
-                nc.scalar.activation(den[:], turned_group_sums(eu_sb[t][:], G), ACT.Identity, bias=1.0)
+                nc.scalar.activation(den[:], turned_group_sums(eu_sb[t][:, cols], G), ACT.Identity, bias=1.0)
             else:
-                vector_group_sums(den[:], eu_sb[t][:], G, 1.0)
+                vector_group_sums(den[:], eu_sb[t][:, cols], G, 1.0)
             rec = small.tile([P, G], F32, name="rec")
             if NEWTON:
                 y0 = small.tile([P, G], F32, name="y0")
@@ -208,59 +232,68 @@ def tile_picked_yschch_net_p_kernel(
                 factor = 1.0 / PRESS
             rr = turn_back(rec[:], G) if PE_TOT else rec[:]
             nc.vector.scalar_tensor_tensor(
-                chs_sb[t][:].rearrange("p (v d) -> p v d", d=D),
-                eu_sb[t][:].rearrange("p (v d) -> p v d", d=D),
+                chs_sb[t][:, cols].rearrange("p (v d) -> p v d", d=D),
+                eu_sb[t][:, cols].rearrange("p (v d) -> p v d", d=D),
                 factor,
                 rr.unsqueeze(2).to_broadcast([P, G, D]),
                 ALU.mult,
                 ALU.mult,
             )
 
-        cs_sb = [keep.tile([P, PACK * n], F32, name="cs%d" % c) for c, n in enumerate(CHUNKS)]
-        gap_sb = [keep.tile([P, PACK * n], F32, name="gap%d" % c) for c, n in enumerate(CHUNKS)]
+        hid_sb = [keep.tile([P, PACK, n], BF16, name="hid%d" % c) for c, n in enumerate(CHUNKS)]
 
-        def sch_cols(c):
-            return sch_sb[:, starts[c] // 16 : (starts[c] + CHUNKS[c]) // 16]
+        gaps = {}
 
-        def fetch_scores(t, c):
-            n = CHUNKS[c]
-            nc.vector.tensor_tensor(
-                gap_sb[c][:, t * n : (t + 1) * n], sc_sb[t][:].indirect(sch_cols(c)), seat_sb[c][:, t, :], ALU.subtract
-            )
-
-        def fetch_choices(t, c):
-            n = CHUNKS[c]
-            nc.scalar.activation(cs_sb[c][:, t * n : (t + 1) * n], chs_sb[t][:].indirect(sch_cols(c)), ACT.Copy)
-
-        def pressure(c):
-            n = CHUNKS[c]
-            fill = small.tile([P, G], F32, name="fill")
-            if PE_FILL:
-                nc.scalar.copy(fill[:, :n], turned_group_sums(cs_sb[c][:], n))
-                ff = turn_back(fill[:, :n], n)
+        def fetch_scores(t, h):
+            cols = slice(h * HALF, (h + 1) * HALF)
+            places = sch_sb[:, h * HALF // 16 : (h + 1) * HALF // 16]
+            gap = work.tile([P, HALF], F32, name="gap", bufs=GAPB)
+            if 2 * t + h >= 2 * PACK - NU:
+                nc.scalar.activation(gap[:], sc_sb[t][:].indirect(places), ACT.Copy)
+                nc.vector.tensor_tensor(gap[:], gap[:], seat_sb[t][:, cols], ALU.subtract)
             else:
-                vector_group_sums(fill[:, :n], cs_sb[c][:], n, 0.0)
-                ff = fill[:, :n]
-            gap = gap_sb[c][:].rearrange("p (v d) -> p v d", d=D)
-            nc.vector.scalar_tensor_tensor(gap, ff.unsqueeze(2).to_broadcast([P, n, D]), PRESS, gap, ALU.mult, ALU.add)
-            nc.vector.scalar_tensor_tensor(gap_sb[c][:], gap_sb[c][:], 0.0, cs_sb[c][:], ALU.max, ALU.subtract)
+                nc.vector.tensor_tensor(gap[:], sc_sb[t][:].indirect(places), seat_sb[t][:, cols], ALU.subtract)
+            gaps[t, h] = gap
+
+        fills = {}
+
+        def fetch_choices(t, h):
+            places = sch_sb[:, h * HALF // 16 : (h + 1) * HALF // 16]
+            cs = work.tile([P, HALF], F32, name="cs", bufs=CSB)
+            nc.scalar.activation(cs[:], chs_sb[t][:].indirect(places), ACT.Copy)
+            fill = small.tile([P, P], F32, name="fill", bufs=CSB)
+            if PE_FILL:
+                nc.scalar.copy(fill[:], turned_group_sums(cs[:], P))
+            else:
+                vector_group_sums(fill[:], cs[:], P, 0.0)
+            fills[t, h] = (cs, fill)
+
+        def pressure(t, h):
+            gap = gaps[t, h]
+            cs, fill = fills[t, h]
+            ff = turn_back(fill[:], P) if PE_FILL else fill[:]
+            gv = gap[:].rearrange("p (v d) -> p v d", d=D)
+            nc.vector.scalar_tensor_tensor(gv, ff.unsqueeze(2).to_broadcast([P, P, D]), PRESS, gv, ALU.mult, ALU.add)
+            nc.vector.scalar_tensor_tensor(gap[:], gap[:], 0.0, cs[:], ALU.max, ALU.subtract)
+            for c, n in enumerate(CHUNKS):
+                if starts[c] // HALF == h:
+                    lo = starts[c] % HALF
+                    nc.scalar.activation(hid_sb[c][:, t, :], gap[:, lo : lo + n], ACT.Copy, scale=gain[:, t : t + 1])
 
         def districts(c):
             n = CHUNKS[c]
-            hid = small.tile([P, PACK, 256], BF16, name="hid")
-            for t in range(PACK):
-                nc.scalar.activation(hid[:, t, :n], gap_sb[c][:, t * n : (t + 1) * n], ACT.Copy, scale=gain[:, t : t + 1])
-            woven = small.tile([P, 256, PACK], BF16, name="woven", align_bytes=64)
-            nc.vector.tensor_copy(
+            hid = hid_sb[c]
+            woven = small.tile([P, HALF, PACK], BF16, name="woven", align_bytes=64)
+            (nc.scalar.copy if c in WEAVE_S else nc.vector.tensor_copy)(
                 out=woven[:, :n, :].rearrange("p (c i) t -> p c t i", i=4),
                 in_=hid[:, :, :n].rearrange("p t (c i) -> p c t i", i=4),
             )
-            codes = small.tile([P, 256], U32, name="codes", align_bytes=64)
-            plane = small.tile([P, 256], U8, name="plane", align_bytes=64)
+            codes = small.tile([P, HALF], U32, name="codes", align_bytes=64)
+            plane = small.tile([P, HALF], U8, name="plane", align_bytes=64)
             nc.vector.quantize_mx(
                 out=codes[:, :n].bitcast(FP8X4), scales=plane[:, :n], in_=woven[:, :n, :].rearrange("p j t -> p (j t)")
             )
-            acc = psum.tile([P, HALF], F32, name="sc_ps")
+            acc = psum.tile([P, HALF], F32, name="sc_ps", bufs=PSA[0])
             nc.tensor.matmul_mx(
                 out=acc[:, :n],
                 lhsT=w3w[:].bitcast(FP4X4),
@@ -270,33 +303,42 @@ def tile_picked_yschch_net_p_kernel(
                 start=True,
                 stop=True,
             )
-            res = small.tile([P, 256], F32, name="res")
+            res = small.tile([P, HALF], F32, name="res")
             nc.scalar.copy(res[:, :n], acc[:, :n])
             nc.sync.dma_start(out=out[:, starts[c] : starts[c] + n], in_=res[:, :n])
 
-        for t in range(PACK + 1):
-            if t < PACK:
-                scores(t, 0)
-            if t >= 1:
-                choices(t - 1)
-            if t < PACK:
-                scores(t, 1)
-                for k, span in enumerate(SPANS):
-                    if span[1] == t + 1:
-                        load_seats(k)
-        w3w = keep.tile([P, 2 * N], U8, name="w3w", tag="w_dealt0", align_bytes=64)
-        w3s = keep.tile([P, N], U8, name="w3s", tag="ws_dealt0", align_bytes=64)
-        unit_sb = keep.tile([P, PACK], F32, name="unit_sb", tag="w_dealt1", align_bytes=64)
-        nc.gpsimd.memset(w3s[:].bitcast(I32), 0)
-        nc.sync.dma_start(out=unit_sb[:], in_=unit.rearrange("(p t) o -> p (t o)", t=PACK))
-        nc.sync.dma_start(out=w3w[:].bitcast(I32), in_=w3_words[0].bitcast(I32))
-        load_scale_rows(nc.sync, w3s, w3_scales)
-        nc.vector.tensor_scalar(gain[:], unit_sb[:], -PRESS, None, ALU.mult)
-        for c in range(len(CHUNKS) + 1):
-            if c < len(CHUNKS):
-                for t in range(PACK):
-                    fetch_scores(t, c)
-                    fetch_choices(t, c)
-                pressure(c)
-            if c >= 1:
-                districts(c - 1)
+        def load_last_weights():
+            w3w = keep.tile([P, 2 * N], U8, name="w3w", tag="w_dealt0", align_bytes=64)
+            w3s = keep.tile([P, N], U8, name="w3s", tag="ws_dealt0", align_bytes=64)
+            nc.gpsimd.memset(w3s[:].bitcast(I32), 0)
+            nc.sync.dma_start(out=w3w[:].bitcast(I32), in_=w3_words[0].bitcast(I32))
+            load_scale_rows([nc.sync] * 4, w3s, w3_scales)
+            return w3w, w3s
+
+        UNITS = 2 * PACK
+        ORDER = [(t, h) for t in range(TM) for h in range(2)] + [(t, h) for h in range(2) for t in range(TM, PACK)]
+        for s in range(UNITS + 12):
+            if s < UNITS:
+                scores(*divmod(s, 2))
+            if s == UNITS - 1:
+                w3w, w3s = load_last_weights()
+            u = s - L1
+            if 0 <= u < UNITS:
+                if PERHALF:
+                    choices(u // 2, (u % 2) * P, P)
+                elif u % 2 == 1:
+                    choices(u // 2, 0, G)
+            u = s - L2
+            if 0 <= u < UNITS:
+                fetch_scores(*ORDER[u])
+            u = s - L3
+            if 0 <= u < UNITS:
+                fetch_choices(*ORDER[u])
+            u = s - L4
+            if 0 <= u < UNITS:
+                t, h = ORDER[u]
+                pressure(t, h)
+                if t == PACK - 1:
+                    for c in range(len(CHUNKS)):
+                        if starts[c] // HALF == h:
+                            districts(c)

@@ -21,26 +21,28 @@ ACT = mybir.ActivationFunctionType
 P = 128
 PACK = 4
 HALF = 512
-CHUNKS = (256,256,256,256)
+CHUNKS = (256,256,256,128,128)
 PRESS = 0.3
 
-GAPB = 4
+GAPB = 6
 CSB = 3
 EUB = 3
-PSA = (2,2,2,2)
-NV = 2
-NU = 0
+PSA = (5,3,1,1)
+NV = 1
+NU = 3
 TM = 2
+REV = False
+PRI = (4, 3, 2, 1, 0)
 L1 = 0
-L2 = 3
-L3 = 5
-L4 = 8
+L2 = 5
+L3 = 6
+L4 = 7
 PERHALF = False
 WB = 3
-SB = 4
-WEAVE_S = (0,)
-PE_TOT = True
-PE_FILL = True
+SB = 3
+WEAVE_S = (1,3)
+PE_TOT = False
+PE_FILL = False
 NEWTON = True
 
 LOG_SLACK = math.log(1.0 / math.log(2.0)) / math.log(2.0) + 1.0 - 1.0 / math.log(2.0)
@@ -72,84 +74,73 @@ def tile_picked_yschch_net_p_kernel(
         offs_sb = keep.tile([P, S // 16], U16, name="offs_sb")
         sch_sb = keep.tile([P, S // 16], U16, name="sch_sb")
         xw = keep.tile([P, T], U32, name="xw")
-        xs = keep.tile([P, T], U8, name="xs", tag="xq", align_bytes=64)
-        w_raw = [keep.tile([P, 2 * H], U8, name="w_raw%d" % a, tag="slot%d" % a) for a in range(2)]
-        ws_raw = [keep.tile([P, H], U8, name="ws_raw0", tag="slot2"), keep.tile([P, H], U8, name="ws_raw1", tag="xb0", align_bytes=64)]
+        xs = keep.tile([P, T], U8, name="xs")
+        w_raw = [keep.tile([P, 2 * H], U8, name="w_raw%d" % a) for a in range(2)]
+        ws_raw = keep.tile([P, 2, H], U8, name="ws_raw")
         w_dealt = [keep.tile([P, 2 * H], U8, name="w_dealt%d" % a, align_bytes=64) for a in range(2)]
-        ws_dealt = [keep.tile([P, H], U8, name="ws_dealt%d" % a, align_bytes=64) for a in range(2)]
+        ws_dealt = keep.tile([P, 2, H], U8, name="ws_dealt", align_bytes=64)
+        w3w = keep.tile([P, 2 * N], U8, name="w3w", align_bytes=64)
+        w3s = keep.tile([P, N], U8, name="w3s", align_bytes=64)
+        unit_sb = keep.tile([P, PACK], F32, name="unit_sb")
+        gain = keep.tile([P, PACK], F32, name="gain")
+        starts = [sum(CHUNKS[:c]) for c in range(len(CHUNKS))]
 
         nc.vector.memset(xs[:].bitcast(I32), 0)
-        nc.gpsimd.memset(ws_raw[1][:].bitcast(I32), 0)
-        nc.gpsimd.memset(ws_raw[0][:].bitcast(I32), 0)
+        for plane in (ws_raw[:].rearrange("p a m -> p (a m)"), w3s[:]):
+            nc.gpsimd.memset(plane.bitcast(I32), 0)
 
         nc.sync.dma_start(offs_sb[:], offs)
-        nc.sync.dma_start(sch_sb[:], sch)
-        unit_sb = keep.tile([P, PACK], F32, name="unit_sb", tag="slot3")
-        nc.sync.dma_start(out=unit_sb[:], in_=unit.rearrange("(p t) o -> p (t o)", t=PACK))
         for a, words in enumerate((w1_words, w2_words)):
             nc.sync.dma_start(out=w_raw[a][:].bitcast(I32), in_=words[0].bitcast(I32))
+        load_scale_rows([nc.sync] * 4, xs, x_scales)
         nc.sync.dma_start(out=xw[:].bitcast(I32), in_=x_words[0].rearrange("p n t -> p (n t)").bitcast(I32))
-        load_scale_rows([nc.scalar] * 4, xs, x_scales)
-        load_scale_rows([nc.gpsimd] + [nc.scalar] * 3, ws_raw[1], w2_scales)
-        load_scale_rows([nc.gpsimd] * 4, ws_raw[0], w1_scales)
-        starts = [sum(CHUNKS[:c]) for c in range(len(CHUNKS))]
+        load_scale_rows([nc.sync] * 4, ws_raw[:, 1, :], w2_scales)
+        load_scale_rows([nc.gpsimd] * 2 + [nc.sync] * 2, ws_raw[:, 0, :], w1_scales)
+        cut_rows = cut.rearrange("(p t) j -> t p j", t=PACK)
+        seat_rows = seat.rearrange("(p t) j -> t p j", t=PACK)
+        cut_sb = [keep.tile([P, S], F32, name="cut%d" % t) for t in range(PACK)]
+        seat_sb = [keep.tile([P, S], F32, name="seat%d" % t) for t in range(PACK)]
+        nc.sync.dma_start(out=cut_sb[0][:], in_=cut_rows[0])
+        nc.sync.dma_start(sch_sb[:], sch)
+        for t in range(PACK):
+            if t + 1 < PACK:
+                nc.sync.dma_start(out=cut_sb[t + 1][:], in_=cut_rows[t + 1])
+            nc.sync.dma_start(out=seat_sb[t][:], in_=seat_rows[t])
+        nc.sync.dma_start(out=unit_sb[:], in_=unit.rearrange("(p t) o -> p (t o)", t=PACK))
+        nc.sync.dma_start(out=w3w[:].bitcast(I32), in_=w3_words[0].bitcast(I32))
+        load_scale_rows([nc.sync] * 4, w3s, w3_scales)
 
         for a in range(2):
             nc.vector.tensor_copy(
                 out=w_dealt[a][:].rearrange("p (t m b) -> p t m b", t=PACK, b=2),
                 in_=w_raw[a][:].rearrange("p (m t b) -> p t m b", t=PACK, b=2),
             )
-
-        gain = keep.tile([P, PACK], F32, name="gain", tag="slot1")
-        nc.scalar.activation(gain[:], unit_sb[:], ACT.Copy, scale=-PRESS)
-
-        def deal_scales(a):
-            nc.vector.tensor_copy(
-                out=ws_dealt[a][:].rearrange("p (t m) -> p t m", t=PACK),
-                in_=ws_raw[a][:].rearrange("p (m t) -> p t m", t=PACK),
-            )
-
-        deal_scales(1)
+        nc.gpsimd.tensor_copy(
+            out=ws_dealt[:].rearrange("p a (t m) -> p a t m", t=PACK),
+            in_=ws_raw[:].rearrange("p a (m t) -> p a t m", t=PACK),
+        )
         xq, xb = [], []
         for h in range(S // HALF):
             cols = offs_sb[:, h * HALF // 16 : (h + 1) * HALF // 16]
             scale_bytes = keep.tile([P, HALF], U8, name="xb%d" % h, align_bytes=64)
             nc.vector.tensor_copy(scale_bytes[:], xs[:].indirect(cols))
             xb.append(scale_bytes)
-        xq_all = keep.tile([P, S], U32, name="xq", align_bytes=64)
         for h in range(S // HALF):
             cols = offs_sb[:, h * HALF // 16 : (h + 1) * HALF // 16]
-            words = xq_all[:, h * HALF : (h + 1) * HALF]
-            nc.vector.tensor_copy(words, xw[:].indirect(cols))
+            words = keep.tile([P, HALF], U32, name="xq%d" % h, align_bytes=64)
+            nc.vector.tensor_copy(words[:], xw[:].indirect(cols))
             xq.append(words)
-            if h == 0:
-                deal_scales(0)
-
-        ident = keep.tile([P, P], F32, name="ident", tag="slot0")
-        make_identity(nc, ident[:])
-        SPANS = ((0, 2), (2, 4))
-        cut_rows = cut.rearrange("(p t) j -> p t j", t=PACK)
-        cut_sb = []
-        for k, (lo, hi) in enumerate(SPANS):
-            tile = keep.tile([P, hi - lo, S], F32, name="cut%d" % k, tag=("slot3", "xw")[k])
-            nc.sync.dma_start(out=tile[:], in_=cut_rows[:, lo:hi, :])
-            cut_sb.extend(tile[:, t, :] for t in range(hi - lo))
-        seat_rows = seat.rearrange("(p t) j -> p t j", t=PACK)
-        seat_sb = []
-
-        def load_seats(lo, hi, tag):
-            tile = keep.tile([P, hi - lo, S], F32, name="seat%d" % lo, tag=tag)
-            nc.sync.dma_start(out=tile[:], in_=seat_rows[:, lo:hi, :])
-            seat_sb.extend(tile[:, t, :] for t in range(hi - lo))
-
-        load_seats(0, 4, "slot2")
+        if PE_TOT or PE_FILL:
+            ident = keep.tile([P, P], F32, name="ident")
+            make_identity(nc, ident[:])
+        nc.gpsimd.tensor_scalar(gain[:], unit_sb[:], -PRESS, 0.0, ALU.mult, ALU.add)
 
         def product(a, t, h, tag):
             acc = psum.tile([P, HALF], F32, name=tag, bufs=PSA[a])
             nc.tensor.matmul_mx(
                 out=acc[:],
                 lhsT=w_dealt[a][:, 2 * P * t : 2 * P * (t + 1)].bitcast(FP4X4),
-                lhsT_scale=ws_dealt[a][:, P * t : P * (t + 1)],
+                lhsT_scale=ws_dealt[:, a, P * t : P * (t + 1)],
                 rhs=xq[h][:].bitcast(FP8X4),
                 rhs_scale=xb[h][:],
                 start=True,
@@ -193,8 +184,8 @@ def tile_picked_yschch_net_p_kernel(
             cols = slice(h * HALF, (h + 1) * HALF)
             if h == 0:
                 eu_sb[t] = small.tile([P, S], F32, name="eu", bufs=EUB)
-            ut_ps = product(1, t, h, "ut_ps")
             sc_ps = product(0, t, h, "sc_ps")
+            ut_ps = product(1, t, h, "ut_ps")
             z = work.tile([P, HALF], F32, name="z")
             nc.vector.tensor_tensor(z[:], sc_ps[:], cut_sb[t][:, cols], ALU.subtract)
             tu = work.tile([P, HALF], F32, name="tu")
@@ -307,38 +298,31 @@ def tile_picked_yschch_net_p_kernel(
             nc.scalar.copy(res[:, :n], acc[:, :n])
             nc.sync.dma_start(out=out[:, starts[c] : starts[c] + n], in_=res[:, :n])
 
-        def load_last_weights():
-            w3w = keep.tile([P, 2 * N], U8, name="w3w", tag="w_dealt0", align_bytes=64)
-            w3s = keep.tile([P, N], U8, name="w3s", tag="ws_dealt0", align_bytes=64)
-            nc.gpsimd.memset(w3s[:].bitcast(I32), 0)
-            nc.sync.dma_start(out=w3w[:].bitcast(I32), in_=w3_words[0].bitcast(I32))
-            load_scale_rows([nc.sync] * 4, w3s, w3_scales)
-            return w3w, w3s
-
         UNITS = 2 * PACK
         ORDER = [(t, h) for t in range(TM) for h in range(2)] + [(t, h) for h in range(2) for t in range(TM, PACK)]
-        for s in range(UNITS + 12):
-            if s < UNITS:
-                scores(*divmod(s, 2))
-            if s == UNITS - 1:
-                w3w, w3s = load_last_weights()
-            u = s - L1
-            if 0 <= u < UNITS:
+        def stage(k, s):
+            u = s - (0, L1, L2, L3, L4)[k]
+            if not 0 <= u < UNITS:
+                return
+            if k == 0:
+                scores(*divmod(u, 2))
+            elif k == 1:
                 if PERHALF:
                     choices(u // 2, (u % 2) * P, P)
                 elif u % 2 == 1:
                     choices(u // 2, 0, G)
-            u = s - L2
-            if 0 <= u < UNITS:
+            elif k == 2:
                 fetch_scores(*ORDER[u])
-            u = s - L3
-            if 0 <= u < UNITS:
+            elif k == 3:
                 fetch_choices(*ORDER[u])
-            u = s - L4
-            if 0 <= u < UNITS:
+            else:
                 t, h = ORDER[u]
                 pressure(t, h)
                 if t == PACK - 1:
                     for c in range(len(CHUNKS)):
                         if starts[c] // HALF == h:
                             districts(c)
+
+        for s in range(UNITS + 12):
+            for k in (PRI if REV else range(5)):
+                stage(k, s)

@@ -25,18 +25,21 @@ CHUNKS = (256,256,256,128,128)
 PRESS = 0.3
 
 GAPB = 6
-CSB = 3
+CSB = 4
 EUB = 3
-PSA = (5,3,1,1)
+PSA = (3,2,2,1)
 NV = 1
-NU = 3
+NU = 2
 TM = 2
 REV = False
 PRI = (4, 3, 2, 1, 0)
+PT = 0
+PF = 8
+L5 = 7
 L1 = 0
 L2 = 5
 L3 = 6
-L4 = 7
+L4 = 8
 PERHALF = False
 WB = 3
 SB = 3
@@ -130,7 +133,7 @@ def tile_picked_yschch_net_p_kernel(
             words = keep.tile([P, HALF], U32, name="xq%d" % h, align_bytes=64)
             nc.vector.tensor_copy(words[:], xw[:].indirect(cols))
             xq.append(words)
-        if PE_TOT or PE_FILL:
+        if PT or PF:
             ident = keep.tile([P, P], F32, name="ident")
             make_identity(nc, ident[:])
         nc.gpsimd.tensor_scalar(gain[:], unit_sb[:], -PRESS, 0.0, ALU.mult, ALU.add)
@@ -171,7 +174,7 @@ def tile_picked_yschch_net_p_kernel(
         def vector_group_sums(dst, values, groups, add):
             pairs = small.tile([P, 2 * (S // D)], F32, name="pairs")
             v = values.rearrange("p (v d) -> p v d", d=D)
-            pv = pairs[:, : 2 * groups].rearrange("p (v e) -> p v e", e=2)
+            pv = pairs[:, : 2 * groups].rearrange("p (e v) -> p v e", e=2)
             nc.vector.tensor_tensor(pv, v[:, :, 0:2], v[:, :, 2:4], ALU.add)
             nc.vector.scalar_tensor_tensor(dst, pv[:, :, 0], add, pv[:, :, 1], ALU.add, ALU.add)
 
@@ -197,11 +200,13 @@ def tile_picked_yschch_net_p_kernel(
             (nc.vector.tensor_copy if 2 * t + h < NV else nc.scalar.copy)(sc_sb[t][:, cols], sc_ps[:])
             nc.vector.scalar_tensor_tensor(eu_sb[t][:, cols], th[:], 1.0, e[:], ALU.add, ALU.mult)
 
+        tots = {}
+
         def choices(t, lo, G):
             cols = slice(lo * D, (lo + G) * D)
             den = small.tile([P, G], F32, name="den")
-            if PE_TOT:
-                nc.scalar.activation(den[:], turned_group_sums(eu_sb[t][:, cols], G), ACT.Identity, bias=1.0)
+            if t < PT:
+                nc.vector.tensor_scalar(den[:], tots[t], 1.0, None, ALU.add)
             else:
                 vector_group_sums(den[:], eu_sb[t][:, cols], G, 1.0)
             rec = small.tile([P, G], F32, name="rec")
@@ -221,7 +226,7 @@ def tile_picked_yschch_net_p_kernel(
             else:
                 nc.vector.reciprocal(rec[:], den[:])
                 factor = 1.0 / PRESS
-            rr = turn_back(rec[:], G) if PE_TOT else rec[:]
+            rr = turn_back(rec[:], G) if t < PT else rec[:]
             nc.vector.scalar_tensor_tensor(
                 chs_sb[t][:, cols].rearrange("p (v d) -> p v d", d=D),
                 eu_sb[t][:, cols].rearrange("p (v d) -> p v d", d=D),
@@ -252,17 +257,21 @@ def tile_picked_yschch_net_p_kernel(
             places = sch_sb[:, h * HALF // 16 : (h + 1) * HALF // 16]
             cs = work.tile([P, HALF], F32, name="cs", bufs=CSB)
             nc.scalar.activation(cs[:], chs_sb[t][:].indirect(places), ACT.Copy)
+            fills[t, h] = (cs, turned_group_sums(cs[:], P) if ORDER.index((t, h)) < PF else None)
+
+        def fill_sums(t, h):
+            cs, turned = fills[t, h]
             fill = small.tile([P, P], F32, name="fill", bufs=CSB)
-            if PE_FILL:
-                nc.scalar.copy(fill[:], turned_group_sums(cs[:], P))
+            if turned is not None:
+                nc.vector.tensor_copy(fill[:], turned)
+                fills[t, h] = (cs, turn_back(fill[:], P))
             else:
                 vector_group_sums(fill[:], cs[:], P, 0.0)
-            fills[t, h] = (cs, fill)
+                fills[t, h] = (cs, fill[:])
 
         def pressure(t, h):
             gap = gaps[t, h]
-            cs, fill = fills[t, h]
-            ff = turn_back(fill[:], P) if PE_FILL else fill[:]
+            cs, ff = fills[t, h]
             gv = gap[:].rearrange("p (v d) -> p v d", d=D)
             nc.vector.scalar_tensor_tensor(gv, ff.unsqueeze(2).to_broadcast([P, P, D]), PRESS, gv, ALU.mult, ALU.add)
             nc.vector.scalar_tensor_tensor(gap[:], gap[:], 0.0, cs[:], ALU.max, ALU.subtract)
@@ -301,11 +310,13 @@ def tile_picked_yschch_net_p_kernel(
         UNITS = 2 * PACK
         ORDER = [(t, h) for t in range(TM) for h in range(2)] + [(t, h) for h in range(2) for t in range(TM, PACK)]
         def stage(k, s):
-            u = s - (0, L1, L2, L3, L4)[k]
+            u = s - (0, L1, L2, L3, L5, L4)[k]
             if not 0 <= u < UNITS:
                 return
             if k == 0:
                 scores(*divmod(u, 2))
+                if u % 2 == 1 and u // 2 < PT:
+                    tots[u // 2] = turned_group_sums(eu_sb[u // 2][:], G)
             elif k == 1:
                 if PERHALF:
                     choices(u // 2, (u % 2) * P, P)
@@ -315,6 +326,8 @@ def tile_picked_yschch_net_p_kernel(
                 fetch_scores(*ORDER[u])
             elif k == 3:
                 fetch_choices(*ORDER[u])
+            elif k == 4:
+                fill_sums(*ORDER[u])
             else:
                 t, h = ORDER[u]
                 pressure(t, h)
@@ -324,5 +337,5 @@ def tile_picked_yschch_net_p_kernel(
                             districts(c)
 
         for s in range(UNITS + 12):
-            for k in (PRI if REV else range(5)):
+            for k in (PRI if REV else range(6)):
                 stage(k, s)

import math
from contextlib import ExitStack

import concourse.mybir as mybir
from concourse.masks import make_identity

K, T, S, D, N, H = 512, 4096, 1024, 4, 128, 512
FLOPS = 2 * K * H * S * 2 + 2 * H * N * S

F32 = mybir.dt.float32
BF16 = mybir.dt.bfloat16
I32 = mybir.dt.int32
U32 = mybir.dt.uint32
U16 = mybir.dt.uint16
U8 = mybir.dt.uint8
FP8X4 = mybir.dt.float8_e4m3fn_x4
FP4X4 = mybir.dt.float4_e2m1fn_x4
ALU = mybir.AluOpType
ACT = mybir.ActivationFunctionType

P = 128
PACK = 4
HALF = 512
CHUNKS = (256,256,256,128,128)
PRESS = 0.3

GAPB = 6
CSB = 4
EUB = 3
PSA = (3,2,2,1)
NV = 1
NU = 2
TM = 2
REV = False
PRI = (4, 3, 2, 1, 0)
PT = 0
PF = 8
L5 = 7
L1 = 0
L2 = 5
L3 = 6
L4 = 8
PERHALF = False
WB = 3
SB = 3
WEAVE_S = (1,3)
PE_TOT = False
PE_FILL = False
NEWTON = True

LOG_SLACK = math.log(1.0 / math.log(2.0)) / math.log(2.0) + 1.0 - 1.0 / math.log(2.0)
SEED_SCALE = -math.log(2.0) / 2.0**23
SEED_BIAS = math.log(2.0) * (127.0 - LOG_SLACK / 2.0)
MID = (2.0 ** (LOG_SLACK / 2.0) + 2.0 ** (-LOG_SLACK / 2.0)) / 2.0
RAD = (2.0 ** (LOG_SLACK / 2.0) - 2.0 ** (-LOG_SLACK / 2.0)) / 2.0
CHEB = 4.0 * (MID / RAD) ** 3 - 3.0 * MID / RAD
QUAD_SCALE = math.sqrt(4.0 / (RAD**3 * CHEB))
QUAD_BIAS = -1.5 * MID * QUAD_SCALE
QUAD_ADD = (12.0 * MID**2 / RAD**3 - 3.0 / RAD) / CHEB - QUAD_BIAS**2


def load_scale_rows(queues, plane, scales):
    for q, queue in enumerate(queues):
        queue.dma_start(out=plane[32 * q : 32 * q + 4, :].bitcast(I32), in_=scales[0, 4 * q : 4 * q + 4, :].bitcast(I32))


def tile_picked_yschch_net_p_kernel(
    tc, x_words, x_scales, w1_words, w1_scales, w2_words, w2_scales, cut, seat, unit, w3_words, w3_scales, offs, sch, out
):
    nc = tc.nc
    with ExitStack() as ctx:
        keep = ctx.enter_context(tc.tile_pool(name="keep", bufs=1))
        work = ctx.enter_context(tc.tile_pool(name="work", bufs=WB))
        small = ctx.enter_context(tc.tile_pool(name="small", bufs=SB))
        psum = ctx.enter_context(tc.psum_pool(name="psum", bufs=2))

        offs_sb = keep.tile([P, S // 16], U16, name="offs_sb")
        sch_sb = keep.tile([P, S // 16], U16, name="sch_sb")
        xw = keep.tile([P, T], U32, name="xw")
        xs = keep.tile([P, T], U8, name="xs")
        w_raw = [keep.tile([P, 2 * H], U8, name="w_raw%d" % a) for a in range(2)]
        ws_raw = keep.tile([P, 2, H], U8, name="ws_raw")
        w_dealt = [keep.tile([P, 2 * H], U8, name="w_dealt%d" % a, align_bytes=64) for a in range(2)]
        ws_dealt = keep.tile([P, 2, H], U8, name="ws_dealt", align_bytes=64)
        w3w = keep.tile([P, 2 * N], U8, name="w3w", align_bytes=64)
        w3s = keep.tile([P, N], U8, name="w3s", align_bytes=64)
        unit_sb = keep.tile([P, PACK], F32, name="unit_sb")
        gain = keep.tile([P, PACK], F32, name="gain")
        starts = [sum(CHUNKS[:c]) for c in range(len(CHUNKS))]

        nc.vector.memset(xs[:].bitcast(I32), 0)
        for plane in (ws_raw[:].rearrange("p a m -> p (a m)"), w3s[:]):
            nc.gpsimd.memset(plane.bitcast(I32), 0)

        nc.sync.dma_start(offs_sb[:], offs)
        for a, words in enumerate((w1_words, w2_words)):
            nc.sync.dma_start(out=w_raw[a][:].bitcast(I32), in_=words[0].bitcast(I32))
        load_scale_rows([nc.sync] * 4, xs, x_scales)
        nc.sync.dma_start(out=xw[:].bitcast(I32), in_=x_words[0].rearrange("p n t -> p (n t)").bitcast(I32))
        load_scale_rows([nc.sync] * 4, ws_raw[:, 1, :], w2_scales)
        load_scale_rows([nc.gpsimd] * 2 + [nc.sync] * 2, ws_raw[:, 0, :], w1_scales)
        cut_rows = cut.rearrange("(p t) j -> t p j", t=PACK)
        seat_rows = seat.rearrange("(p t) j -> t p j", t=PACK)
        cut_sb = [keep.tile([P, S], F32, name="cut%d" % t) for t in range(PACK)]
        seat_sb = [keep.tile([P, S], F32, name="seat%d" % t) for t in range(PACK)]
        nc.sync.dma_start(out=cut_sb[0][:], in_=cut_rows[0])
        nc.sync.dma_start(sch_sb[:], sch)
        for t in range(PACK):
            if t + 1 < PACK:
                nc.sync.dma_start(out=cut_sb[t + 1][:], in_=cut_rows[t + 1])
            nc.sync.dma_start(out=seat_sb[t][:], in_=seat_rows[t])
        nc.sync.dma_start(out=unit_sb[:], in_=unit.rearrange("(p t) o -> p (t o)", t=PACK))
        nc.sync.dma_start(out=w3w[:].bitcast(I32), in_=w3_words[0].bitcast(I32))
        load_scale_rows([nc.sync] * 4, w3s, w3_scales)

        for a in range(2):
            nc.vector.tensor_copy(
                out=w_dealt[a][:].rearrange("p (t m b) -> p t m b", t=PACK, b=2),
                in_=w_raw[a][:].rearrange("p (m t b) -> p t m b", t=PACK, b=2),
            )
        nc.gpsimd.tensor_copy(
            out=ws_dealt[:].rearrange("p a (t m) -> p a t m", t=PACK),
            in_=ws_raw[:].rearrange("p a (m t) -> p a t m", t=PACK),
        )
        xq, xb = [], []
        for h in range(S // HALF):
            cols = offs_sb[:, h * HALF // 16 : (h + 1) * HALF // 16]
            scale_bytes = keep.tile([P, HALF], U8, name="xb%d" % h, align_bytes=64)
            nc.vector.tensor_copy(scale_bytes[:], xs[:].indirect(cols))
            xb.append(scale_bytes)
        for h in range(S // HALF):
            cols = offs_sb[:, h * HALF // 16 : (h + 1) * HALF // 16]
            words = keep.tile([P, HALF], U32, name="xq%d" % h, align_bytes=64)
            nc.vector.tensor_copy(words[:], xw[:].indirect(cols))
            xq.append(words)
        if PT or PF:
            ident = keep.tile([P, P], F32, name="ident")
            make_identity(nc, ident[:])
        nc.gpsimd.tensor_scalar(gain[:], unit_sb[:], -PRESS, 0.0, ALU.mult, ALU.add)

        def product(a, t, h, tag):
            acc = psum.tile([P, HALF], F32, name=tag, bufs=PSA[a])
            nc.tensor.matmul_mx(
                out=acc[:],
                lhsT=w_dealt[a][:, 2 * P * t : 2 * P * (t + 1)].bitcast(FP4X4),
                lhsT_scale=ws_dealt[:, a, P * t : P * (t + 1)],
                rhs=xq[h][:].bitcast(FP8X4),
                rhs_scale=xb[h][:],
                start=True,
                stop=True,
            )
            return acc

        def turned_group_sums(values, groups):
            turned = psum.tile([P, HALF], F32, name="turned", bufs=PSA[2])
            for b in range(groups // P):
                for d in range(D):
                    nc.tensor.matmul(
                        turned[:, P * b : P * (b + 1)],
                        lhsT=values[:, D * P * b + d : D * P * (b + 1) : D],
                        rhs=ident[:],
                        is_transpose=True,
                        start=(d == 0),
                        stop=(d == D - 1),
                    )
            return turned[:, :groups]

        def turn_back(values, groups):
            back = psum.tile([P, HALF], F32, name="back", bufs=PSA[3])
            for b in range(groups // P):
                nc.tensor.transpose(back[:, P * b : P * (b + 1)], values[:, P * b : P * (b + 1)], ident[:])
            return back[:, :groups]

        def vector_group_sums(dst, values, groups, add):
            pairs = small.tile([P, 2 * (S // D)], F32, name="pairs")
            v = values.rearrange("p (v d) -> p v d", d=D)
            pv = pairs[:, : 2 * groups].rearrange("p (e v) -> p v e", e=2)
            nc.vector.tensor_tensor(pv, v[:, :, 0:2], v[:, :, 2:4], ALU.add)
            nc.vector.scalar_tensor_tensor(dst, pv[:, :, 0], add, pv[:, :, 1], ALU.add, ALU.add)

        sc_sb = [keep.tile([P, S], F32, name="sc%d" % t) for t in range(PACK)]
        chs_sb = [keep.tile([P, S], F32, name="chs%d" % t) for t in range(PACK)]
        eu_sb = [None] * PACK
        G = S // D

        def scores(t, h):
            cols = slice(h * HALF, (h + 1) * HALF)
            if h == 0:
                eu_sb[t] = small.tile([P, S], F32, name="eu", bufs=EUB)
            sc_ps = product(0, t, h, "sc_ps")
            ut_ps = product(1, t, h, "ut_ps")
            z = work.tile([P, HALF], F32, name="z")
            nc.vector.tensor_tensor(z[:], sc_ps[:], cut_sb[t][:, cols], ALU.subtract)
            tu = work.tile([P, HALF], F32, name="tu")
            nc.scalar.activation(tu[:], ut_ps[:], ACT.Tanh)
            e = work.tile([P, HALF], F32, name="e")
            nc.scalar.activation(e[:], tu[:], ACT.Exp, scale=0.9)
            th = work.tile([P, HALF], F32, name="th")
            nc.scalar.activation(th[:], z[:], ACT.Tanh, scale=1.5)
            (nc.vector.tensor_copy if 2 * t + h < NV else nc.scalar.copy)(sc_sb[t][:, cols], sc_ps[:])
            nc.vector.scalar_tensor_tensor(eu_sb[t][:, cols], th[:], 1.0, e[:], ALU.add, ALU.mult)

        tots = {}

        def choices(t, lo, G):
            cols = slice(lo * D, (lo + G) * D)
            den = small.tile([P, G], F32, name="den")
            if t < PT:
                nc.vector.tensor_scalar(den[:], tots[t], 1.0, None, ALU.add)
            else:
                vector_group_sums(den[:], eu_sb[t][:, cols], G, 1.0)
            rec = small.tile([P, G], F32, name="rec")
            if NEWTON:
                y0 = small.tile([P, G], F32, name="y0")
                nc.scalar.activation(y0[:], den[:].bitcast(U32), ACT.Exp, scale=SEED_SCALE, bias=SEED_BIAS)
                t0 = small.tile([P, G], F32, name="t0")
                nc.vector.tensor_tensor(t0[:], den[:], y0[:], ALU.mult)
                q = small.tile([P, G], F32, name="q")
                nc.scalar.activation(q[:], t0[:], ACT.Square, scale=QUAD_SCALE, bias=QUAD_BIAS)
                y1 = small.tile([P, G], F32, name="y1")
                nc.vector.scalar_tensor_tensor(y1[:], q[:], QUAD_ADD, y0[:], ALU.add, ALU.mult)
                t1 = small.tile([P, G], F32, name="t1")
                nc.vector.tensor_tensor(t1[:], den[:], y1[:], ALU.mult)
                nc.vector.scalar_tensor_tensor(rec[:], t1[:], 2.0, y1[:], ALU.subtract, ALU.mult)
                factor = -1.0 / PRESS
            else:
                nc.vector.reciprocal(rec[:], den[:])
                factor = 1.0 / PRESS
            rr = turn_back(rec[:], G) if t < PT else rec[:]
            nc.vector.scalar_tensor_tensor(
                chs_sb[t][:, cols].rearrange("p (v d) -> p v d", d=D),
                eu_sb[t][:, cols].rearrange("p (v d) -> p v d", d=D),
                factor,
                rr.unsqueeze(2).to_broadcast([P, G, D]),
                ALU.mult,
                ALU.mult,
            )

        hid_sb = [keep.tile([P, PACK, n], BF16, name="hid%d" % c) for c, n in enumerate(CHUNKS)]

        gaps = {}

        def fetch_scores(t, h):
            cols = slice(h * HALF, (h + 1) * HALF)
            places = sch_sb[:, h * HALF // 16 : (h + 1) * HALF // 16]
            gap = work.tile([P, HALF], F32, name="gap", bufs=GAPB)
            if 2 * t + h >= 2 * PACK - NU:
                nc.scalar.activation(gap[:], sc_sb[t][:].indirect(places), ACT.Copy)
                nc.vector.tensor_tensor(gap[:], gap[:], seat_sb[t][:, cols], ALU.subtract)
            else:
                nc.vector.tensor_tensor(gap[:], sc_sb[t][:].indirect(places), seat_sb[t][:, cols], ALU.subtract)
            gaps[t, h] = gap

        fills = {}

        def fetch_choices(t, h):
            places = sch_sb[:, h * HALF // 16 : (h + 1) * HALF // 16]
            cs = work.tile([P, HALF], F32, name="cs", bufs=CSB)
            nc.scalar.activation(cs[:], chs_sb[t][:].indirect(places), ACT.Copy)
            fills[t, h] = (cs, turned_group_sums(cs[:], P) if ORDER.index((t, h)) < PF else None)

        def fill_sums(t, h):
            cs, turned = fills[t, h]
            fill = small.tile([P, P], F32, name="fill", bufs=CSB)
            if turned is not None:
                nc.vector.tensor_copy(fill[:], turned)
                fills[t, h] = (cs, turn_back(fill[:], P))
            else:
                vector_group_sums(fill[:], cs[:], P, 0.0)
                fills[t, h] = (cs, fill[:])

        def pressure(t, h):
            gap = gaps[t, h]
            cs, ff = fills[t, h]
            gv = gap[:].rearrange("p (v d) -> p v d", d=D)
            nc.vector.scalar_tensor_tensor(gv, ff.unsqueeze(2).to_broadcast([P, P, D]), PRESS, gv, ALU.mult, ALU.add)
            nc.vector.scalar_tensor_tensor(gap[:], gap[:], 0.0, cs[:], ALU.max, ALU.subtract)
            for c, n in enumerate(CHUNKS):
                if starts[c] // HALF == h:
                    lo = starts[c] % HALF
                    nc.scalar.activation(hid_sb[c][:, t, :], gap[:, lo : lo + n], ACT.Copy, scale=gain[:, t : t + 1])

        def districts(c):
            n = CHUNKS[c]
            hid = hid_sb[c]
            woven = small.tile([P, HALF, PACK], BF16, name="woven", align_bytes=64)
            (nc.scalar.copy if c in WEAVE_S else nc.vector.tensor_copy)(
                out=woven[:, :n, :].rearrange("p (c i) t -> p c t i", i=4),
                in_=hid[:, :, :n].rearrange("p t (c i) -> p c t i", i=4),
            )
            codes = small.tile([P, HALF], U32, name="codes", align_bytes=64)
            plane = small.tile([P, HALF], U8, name="plane", align_bytes=64)
            nc.vector.quantize_mx(
                out=codes[:, :n].bitcast(FP8X4), scales=plane[:, :n], in_=woven[:, :n, :].rearrange("p j t -> p (j t)")
            )
            acc = psum.tile([P, HALF], F32, name="sc_ps", bufs=PSA[0])
            nc.tensor.matmul_mx(
                out=acc[:, :n],
                lhsT=w3w[:].bitcast(FP4X4),
                lhsT_scale=w3s[:],
                rhs=codes[:, :n].bitcast(FP8X4),
                rhs_scale=plane[:, :n],
                start=True,
                stop=True,
            )
            res = small.tile([P, HALF], F32, name="res")
            nc.scalar.copy(res[:, :n], acc[:, :n])
            nc.sync.dma_start(out=out[:, starts[c] : starts[c] + n], in_=res[:, :n])

        UNITS = 2 * PACK
        ORDER = [(t, h) for t in range(TM) for h in range(2)] + [(t, h) for h in range(2) for t in range(TM, PACK)]
        def stage(k, s):
            u = s - (0, L1, L2, L3, L5, L4)[k]
            if not 0 <= u < UNITS:
                return
            if k == 0:
                scores(*divmod(u, 2))
                if u % 2 == 1 and u // 2 < PT:
                    tots[u // 2] = turned_group_sums(eu_sb[u // 2][:], G)
            elif k == 1:
                if PERHALF:
                    choices(u // 2, (u % 2) * P, P)
                elif u % 2 == 1:
                    choices(u // 2, 0, G)
            elif k == 2:
                fetch_scores(*ORDER[u])
            elif k == 3:
                fetch_choices(*ORDER[u])
            elif k == 4:
                fill_sums(*ORDER[u])
            else:
                t, h = ORDER[u]
                pressure(t, h)
                if t == PACK - 1:
                    for c in range(len(CHUNKS)):
                        if starts[c] // HALF == h:
                            districts(c)

        for s in range(UNITS + 12):
            for k in (PRI if REV else range(6)):
                stage(k, s)
